import numpy as np
import ml_dtypes


def mxq(x, axis, fmt="e4m3"):
    dtype, down = {"e4m3": (ml_dtypes.float8_e4m3fn, 7), "e5m2": (ml_dtypes.float8_e5m2, 14)}[fmt]
    v = np.moveaxis(np.asarray(x, np.float32).astype(ml_dtypes.bfloat16).astype(np.float64), axis, -1)
    blocks = v.reshape(v.shape[:-1] + (-1, 32))
    amax = np.abs(blocks).max(-1, keepdims=True)
    byte = np.maximum(np.where(amax > 0, np.frexp(amax)[1] - 1 + 127, 0) - down, 1)
    scale = np.exp2(byte - 127.0)
    codes = (blocks / scale).astype(np.float32).astype(dtype).astype(np.float64)
    return np.moveaxis((codes * scale).reshape(v.shape), -1, axis)


WIDE = False


def mx_kscale(k):
    if not WIDE:
        return np.ones(k)
    levels = np.array([10, -10, 5, -5, 0])
    if k % 512:
        return np.exp2(np.random.permutation(np.resize(levels, k // 32))).repeat(32)
    a = np.empty((k // 512, 16))
    for p in range(k // 512):
        a[p, :8] = np.random.permutation(np.resize(levels, 8))
        for g in range(8):
            far = levels[np.abs(levels - a[p, g]) >= 10]
            a[p, g + 8] = far[np.random.randint(len(far))]
    return np.exp2(a.ravel()).repeat(32)


def f64(x):
    return np.asarray(x).astype(np.float64)


def striped(idx):
    return np.tile(idx.reshape(-1, 16).T, (8, 1)).astype(np.uint16)


def unstriped(offs):
    return offs[:16].T.reshape(-1).astype(np.int64)


E2M1 = np.array([0.0, 0.5, 1.0, 1.5, 2.0, 3.0, 4.0, 6.0, -0.0, -0.5, -1.0, -1.5, -2.0, -3.0, -4.0, -6.0])


def pack_weight(w, fmt):
    k, n = w.shape
    w = f64(np.asarray(w, np.float32).astype(ml_dtypes.bfloat16)).reshape(k // 32, 32, n)
    amax = np.abs(w).max(1)
    if fmt == "e4m3":
        byte = np.frexp(amax)[1] - 1 + 127 - 7
    else:
        mant, ex = np.frexp(amax / 6.0)
        byte = np.where(mant > 0.5, ex, ex - 1) + 127
    byte = np.clip(np.where(amax > 0, byte, 1), 1, 254)
    scaled = (w * np.exp2(127.0 - byte)[:, None, :]).reshape(k, n).astype(np.float32)
    by_word = np.ascontiguousarray(scaled.reshape(k // 512, 128, 4, n).transpose(0, 1, 3, 2))
    if fmt == "e4m3":
        words = by_word.astype(ml_dtypes.float8_e4m3fn).view(np.uint8)
    else:
        c = by_word.astype(ml_dtypes.float4_e2m1fn).view(np.uint8) & 0xF
        words = (c[..., 0::2] | (c[..., 1::2] << 4)).reshape(k // 512, 128, 2 * n)
    return np.ascontiguousarray(words), np.ascontiguousarray(byte.astype(np.uint8).reshape(k // 512, 16, n))


def unpack_weight(words, scales, fmt):
    g, _, n = scales.shape
    words = np.ascontiguousarray(words).reshape(g, 128, n, -1)
    if fmt == "e4m3":
        vals = words.view(ml_dtypes.float8_e4m3fn).astype(np.float64)
    else:
        nib = np.empty((g, 128, n, 4), np.uint8)
        nib[..., 0::2] = words & 0xF
        nib[..., 1::2] = words >> 4
        vals = E2M1[nib]
    vals = vals * np.repeat(np.exp2(scales.astype(np.float64) - 127.0), 8, axis=1)[..., None]
    return vals.transpose(0, 1, 3, 2).reshape(g * 512, n)


def d_silu(v):
    s = 1.0 / (1.0 + np.exp(-np.maximum(v, -700.0)))
    return s * (1.0 + v * (1.0 - s))


K, T, E, C, H, N = 512, 768, 6, 256, 512, 512


def by_expert(wq, xq):
    return np.concatenate([wq[e].T @ xq[:, e * C:(e + 1) * C] for e in range(E)], axis=1)


def setup_inputs():
    n = np.random.standard_normal
    s = mx_kscale(K)
    v = mx_kscale(N)
    u = mx_kscale(H)
    first = np.random.permutation(np.repeat(np.arange(E), T // E))
    second = (first + 1 + np.random.permutation(np.repeat(np.arange(E - 1), -(-T // (E - 1)))[:T])) % E
    while np.bincount(second, minlength=E).max() != T // E:
        load = np.bincount(second, minlength=E); hi, lo = int(load.argmax()), int(load.argmin())
        t = np.flatnonzero((second == hi) & (first != lo))[0]; second[t] = lo
    slot_token = np.empty(E * C, np.int64); pos = np.empty((2, T), np.int64); fill = np.zeros(E, np.int64)
    place = np.stack([np.random.permutation(C) for _ in range(E)])
    for r, deal in enumerate((first, second)):
        for t in np.random.permutation(T):
            e = deal[t]; j = e * C + place[e, fill[e]]; fill[e] += 1; slot_token[j] = t; pos[r, t] = j
    g = np.random.uniform(0.2, 0.8, T)
    w_slot = np.empty(E * C); w_slot[pos[0]] = g; w_slot[pos[1]] = 1.0 - g
    x = pack_weight(n((K, T)) * s[:, None], "e4m3")
    dy = pack_weight(n((N, T)) * v[:, None], "e4m3")
    m1 = n((E, K, H))
    w1 = [pack_weight(m, "e2m1") for m in m1 / np.sqrt(K) / s[None, :, None]]
    w2t = [pack_weight(m, "e2m1") for m in n((E, N, H)) / np.sqrt(N) / v[None, :, None] * u]
    w1t = [pack_weight(m, "e2m1") for m in m1.transpose(0, 2, 1) / np.sqrt(H) / u[None, :, None]]
    return {
        "x_words": x[0],
        "x_scales": x[1],
        "dy_words": dy[0],
        "dy_scales": dy[1],
        "w1_words": np.stack([m[0] for m in w1]),
        "w1_scales": np.stack([m[1] for m in w1]),
        "w2t_words": np.stack([m[0] for m in w2t]),
        "w2t_scales": np.stack([m[1] for m in w2t]),
        "w1t_words": np.stack([m[0] for m in w1t]),
        "w1t_scales": np.stack([m[1] for m in w1t]),
        "gate": (np.tile(w_slot, (128, 1))).astype(np.float32),
        "offs": striped(slot_token),
        "pos1": striped(pos[0]),
        "pos2": striped(pos[1]),
    }


def reference(x_words, x_scales, dy_words, dy_scales, w1_words, w1_scales, w2t_words, w2t_scales, w1t_words, w1t_scales, gate, offs, pos1, pos2):
    w1 = np.stack([unpack_weight(w1_words[e], w1_scales[e], "e2m1") for e in range(E)])
    w2t = np.stack([unpack_weight(w2t_words[e], w2t_scales[e], "e2m1") for e in range(E)])
    w1t = np.stack([unpack_weight(w1t_words[e], w1t_scales[e], "e2m1") for e in range(E)])
    idx = unstriped(offs)
    xq = unpack_weight(x_words, x_scales, "e4m3")[:, idx]
    gq = unpack_weight(dy_words, dy_scales, "e4m3")[:, idx]
    dh = f64(gate[:1]) * by_expert(w2t, gq)
    a = by_expert(w1, xq)
    dx = by_expert(w1t, mxq(dh * d_silu(a), 0, "e4m3"))
    out = dx[:, unstriped(pos1)] + dx[:, unstriped(pos2)]
    return out

@@ -1,0 +1,303 @@
+from contextlib import ExitStack
+
+import concourse.mybir as mybir
+from concourse.masks import make_identity
+
+K, T, E, C, H, N = 512, 768, 6, 256, 512, 512
+S = E * C
+FLOPS = 3 * 2 * 512 * 512 * S
+
+F32 = mybir.dt.float32
+BF16 = mybir.dt.bfloat16
+I32 = mybir.dt.int32
+U32 = mybir.dt.uint32
+U16 = mybir.dt.uint16
+U8 = mybir.dt.uint8
+FP8X4 = mybir.dt.float8_e4m3fn_x4
+FP4X4 = mybir.dt.float4_e2m1fn_x4
+ACT = mybir.ActivationFunctionType
+ALU = mybir.AluOpType
+
+P = 128
+LIST_ROWS = 16
+BLOCKS = C // P
+WORD_BYTES = 2
+EARLY = 2
+MODES = "AAAAAAAAAAAA"
+ADDS = "VVVV"
+TEV = "SSSSSS"
+GROUPS = (0, 1, 2, 3, 4, 5, 6)
+WIDE = "000000"
+SPLIT = 1
+HEAD = 1
+
+
+def tile_moe_rec_mlp_silu_kernel(
+    tc, x_words, x_scales, dy_words, dy_scales, w1_words, w1_scales, w2t_words, w2t_scales,
+    w1t_words, w1t_scales, gate, offs, pos1, pos2, out,
+):
+    nc = tc.nc
+    with ExitStack() as ctx:
+        keep = ctx.enter_context(tc.tile_pool(name="keep", bufs=1))
+        work = ctx.enter_context(tc.tile_pool(name="work", bufs=4))
+        picked = ctx.enter_context(tc.tile_pool(name="picked", bufs=1))
+
+        offs_t = keep.tile([P, S // LIST_ROWS], U16, name="offs_t")
+        pos1_t = keep.tile([P, T // LIST_ROWS], U16, name="pos1_t")
+        pos2_t = keep.tile([P, T // LIST_ROWS], U16, name="pos2_t")
+        xw = keep.tile([P, T], I32, name="xw", align_bytes=64)
+        yw = keep.tile([P, T], I32, name="yw", align_bytes=64)
+        xs = keep.tile([P, T], U8, name="xs", align_bytes=64)
+        ys = keep.tile([P, T], U8, name="ys", align_bytes=64)
+        w1s = keep.tile([P, E * H], U8, name="w1s", align_bytes=64)
+        w2s = keep.tile([P, E * H], U8, name="w2s", align_bytes=64)
+        w3s = keep.tile([P, E * K], U8, name="w3s", align_bytes=64)
+        gate_rows = keep.tile([P, P], F32, name="gate_rows")
+        gate_cols = keep.tile([P, E * BLOCKS], F32, name="gate_cols")
+        ident = keep.tile([P, P], F32, name="ident")
+        warm_in = keep.tile([P, 1], F32, name="warm_in")
+        warm_out = keep.tile([P, 1], F32, name="warm_out")
+
+        nc.vector.memset(warm_in[:], 0.0)
+        nc.scalar.activation(warm_out[:], warm_in[:], ACT.Silu)
+        for plane in (xs, ys):
+            nc.gpsimd.memset(plane[:].bitcast(I32), 0)
+        for plane in (w1s, w2s, w3s):
+            nc.vector.memset(plane[:].bitcast(I32), 0)
+
+        def load_token_words(t, words):
+            nc.sync.dma_start(t[:], words[0].rearrange("p t d -> p (t d)").bitcast(I32))
+
+        def load_token_scales(plane, scales):
+            for r in range(4):
+                nc.sync.dma_start(plane[:].bitcast(I32)[r:P:32, :], scales[0, r:16:4, :].bitcast(I32))
+
+        def load_weight_scales(plane, scales):
+            for r in range(4):
+                nc.sync.dma_start(
+                    plane[:].bitcast(I32)[r:P:32, :].rearrange("q (e n) -> q e n", e=E),
+                    scales[:, 0, r:16:4, :].rearrange("e q n -> q e n").bitcast(I32),
+                )
+
+        def load_weight_words(queue, words, e0, e1, name):
+            t = keep.tile([P, e1 - e0, H * WORD_BYTES], U8, name=name, align_bytes=64)
+            queue.dma_start(t[:].bitcast(I32), words[e0:e1, 0].rearrange("e p n -> p e n").bitcast(I32))
+            return [t[:, e, :] for e in range(e1 - e0)]
+
+        gate_src = gate.rearrange("a (b p) -> (a b) p", p=P)[0:P, :]
+        nc.sync.dma_start(offs_t[:], offs)
+        load_token_words(xw, x_words)
+        if HEAD == 1:
+            w1w = load_weight_words(nc.sync, w1_words, 0, EARLY, "w1_early")
+            load_token_words(yw, dy_words)
+            load_token_scales(xs, x_scales)
+            load_weight_scales(w1s, w1_scales)
+            load_token_scales(ys, dy_scales)
+            load_weight_scales(w2s, w2t_scales)
+            w2w = load_weight_words(nc.sync, w2t_words, 0, EARLY, "w2_early")
+            nc.sync.dma_start(gate_rows[:], gate_src)
+            make_identity(nc, ident[:])
+        else:
+            w1w = load_weight_words(nc.gpsimd, w1_words, 0, EARLY, "w1_early")
+            w2w = load_weight_words(nc.gpsimd, w2t_words, 0, EARLY, "w2_early")
+            nc.gpsimd.dma_start(gate_rows[:], gate_src)
+            make_identity(nc, ident[:])
+            load_token_scales(xs, x_scales)
+            load_weight_scales(w1s, w1_scales)
+            load_token_words(yw, dy_words)
+            load_token_scales(ys, dy_scales)
+            load_weight_scales(w2s, w2t_scales)
+        w1w = w1w + load_weight_words(nc.sync, w1_words, EARLY, E, "w1_late")
+        w2w = w2w + load_weight_words(nc.sync, w2t_words, EARLY, E, "w2_late")
+        load_weight_scales(w3s, w1t_scales)
+        w3w = load_weight_words(nc.sync, w1t_words, 0, E, "w3_all")
+        nc.sync.dma_start(pos1_t[:], pos1)
+        nc.sync.dma_start(pos2_t[:], pos2)
+
+        dx = [keep.tile([P, S], F32, name="dx%d" % kb) for kb in range(K // P)]
+        codes, scales = [], []
+
+        def back(e, kb, bank):
+            nc.tensor.matmul_mx(
+                bank,
+                lhsT=w3w[e][:, kb * P * WORD_BYTES : (kb + 1) * P * WORD_BYTES].bitcast(FP4X4),
+                lhsT_scale=w3s[:, e * K + kb * P : e * K + (kb + 1) * P],
+                rhs=codes[e][:].bitcast(FP8X4), rhs_scale=scales[e][:], start=True, stop=True,
+            )
+
+        def by_word_parity(bank):
+            return bank[:].rearrange("s (p u d) -> s u p d", u=2, d=2)
+
+        def three(t):
+            return t[:].rearrange("s (u p d) -> s u p d", u=2, d=2)
+
+        with tc.psum_pool(name="psum", bufs=2) as psum:
+            gate_ps = psum.tile([P, 4, P], F32, name="turn", tag="turn", bufs=2)
+            nc.tensor.transpose(gate_ps[:, 0, :], gate_rows[:], ident[:])
+            nc.vector.tensor_scalar(gate_cols[:], gate_ps[:, 0, 0 : E * BLOCKS], -0.5, None, ALU.mult)
+
+            picks, das, turns, stage = {}, {}, {}, {}
+
+            def gather(e):
+                if e not in GROUPS:
+                    return
+                e1 = GROUPS[GROUPS.index(e) + 1]
+                n = (e1 - e) * C
+                slots = offs_t[:, e * C // LIST_ROWS : e1 * C // LIST_ROWS]
+                xg = picked.tile([P, n], U32, name="xg", align_bytes=64, bufs=2)
+                xgs = picked.tile([P, n], U8, name="xgs", align_bytes=64, bufs=2)
+                yg = picked.tile([P, n], U32, name="yg", align_bytes=64, bufs=2)
+                ygs = picked.tile([P, n], U8, name="ygs", align_bytes=64, bufs=2)
+                nc.vector.tensor_copy(xg[:], xw[:].bitcast(U32).indirect(slots))
+                nc.vector.tensor_copy(xgs[:], xs[:].indirect(slots))
+                nc.vector.tensor_copy(yg[:], yw[:].bitcast(U32).indirect(slots))
+                nc.vector.tensor_copy(ygs[:], ys[:].indirect(slots))
+                for i in range(e, e1):
+                    picks[i] = [t[:, (i - e) * C : (i - e + 1) * C] for t in (xg, xgs, yg, ygs)]
+
+            def gradient(j):
+                e, b = divmod(j, BLOCKS)
+                xg, xgs, yg, ygs = picks[e]
+                mode = MODES[j]
+                gcol = gate_cols[:, j : j + 1]
+                cols = slice(b * P, (b + 1) * P)
+                a_ps = psum.tile([P, H], F32, name="a_ps", bufs=3)
+                nc.tensor.matmul_mx(
+                    a_ps[:], lhsT=xg[:, cols].bitcast(FP8X4), lhsT_scale=xgs[:, cols],
+                    rhs=w1w[e].bitcast(FP4X4), rhs_scale=w1s[:, e * H : (e + 1) * H], start=True, stop=True,
+                )
+                h_ps = psum.tile([P, H], F32, name="h_ps", bufs=2)
+                nc.tensor.matmul_mx(
+                    h_ps[:], lhsT=yg[:, cols].bitcast(FP8X4), lhsT_scale=ygs[:, cols],
+                    rhs=w2w[e].bitcast(FP4X4), rhs_scale=w2s[:, e * H : (e + 1) * H], start=True, stop=True,
+                )
+                if b == 0:
+                    stage[e] = [work.tile([P, BLOCKS * H], F32, name=n, bufs=3) for n in ("silu", "tanh", "third", "part")]
+                    stage[e].append(work.tile([P, BLOCKS * H], BF16, name="da", bufs=3))
+                silu, tanh, third, part, da = [t[:, b * H : (b + 1) * H] for t in stage[e]]
+                words = da.bitcast(F32)
+                wide = WIDE[e] == "1"
+                w_silu, w_tanh, w_third, w_part, w_da = stage[e]
+                if mode in "AF":
+                    nc.scalar.activation(three(silu), by_word_parity(a_ps), ACT.Silu, scale=-1.0)
+                    nc.scalar.activation(three(tanh), by_word_parity(a_ps), ACT.Tanh, scale=0.5)
+                    if mode == "A":
+                        nc.scalar.activation(three(third), by_word_parity(h_ps), ACT.Copy, scale=gcol)
+                        if not wide:
+                            nc.vector.scalar_tensor_tensor(part[:], tanh[:], 1.0, third[:], ALU.add, ALU.mult)
+                        elif b == 1:
+                            nc.vector.scalar_tensor_tensor(w_part[:], w_tanh[:], 1.0, w_third[:], ALU.add, ALU.mult)
+                    else:
+                        nc.vector.tensor_scalar(third[:], tanh[:], 1.0, gcol, ALU.add, ALU.mult)
+                        nc.vector.tensor_tensor(three(part), three(third), by_word_parity(h_ps), ALU.mult)
+                    if not wide:
+                        nc.vector.scalar_tensor_tensor(da[:], silu[:], 1.0, part[:], ALU.subtract, ALU.mult)
+                    elif b == 1:
+                        nc.vector.scalar_tensor_tensor(w_da[:], w_silu[:], 1.0, w_part[:], ALU.subtract, ALU.mult)
+                    das[j] = [words[:, u * P : (u + 1) * P] for u in range(2)]
+                else:
+                    nc.scalar.activation(silu[:], a_ps[:], ACT.Silu, scale=-1.0)
+                    nc.scalar.activation(tanh[:], a_ps[:], ACT.Tanh, scale=0.5)
+                    if mode in "CD":
+                        nc.gpsimd.tensor_scalar(third[:], tanh[:], 1.0, gcol, ALU.add, ALU.mult)
+                    else:
+                        nc.scalar.activation(third[:], tanh[:], ACT.Identity, scale=gcol, bias=gcol)
+                    nc.vector.scalar_tensor_tensor(part[:], silu[:], 1.0, h_ps[:], ALU.subtract, ALU.mult)
+                    last = nc.gpsimd if mode in "BC" else nc.vector
+                    if not wide:
+                        last.tensor_tensor(da[:], part[:], third[:], ALU.mult)
+                    elif b == 1:
+                        last.tensor_tensor(w_da[:], w_part[:], w_third[:], ALU.mult)
+                    das[j] = [words[:, u : 2 * P : 2] for u in range(2)]
+
+            def turn_block(j):
+                e, b = divmod(j, BLOCKS)
+                if b == 0:
+                    turns[e] = psum.tile([P, BLOCKS, 2, P], F32, name="turn", tag="turn", bufs=2)
+                for u in range(2):
+                    nc.tensor.transpose(turns[e][:, b, u, :], das[j][u], ident[:])
+
+            def quantise(e):
+                grouped = work.tile([P, C * 4], BF16, name="grouped", align_bytes=64)
+                to = grouped[:].bitcast(F32).rearrange("p (b s u) -> p b s u", b=BLOCKS, u=2)
+                if TEV[e] == "S":
+                    nc.scalar.copy(to, turns[e][:].rearrange("p b u s -> p b s u"))
+                else:
+                    nc.vector.tensor_copy(to, turns[e][:].rearrange("p b u s -> p b s u"))
+                codes.append(keep.tile([P, C], U32, name="codes%d" % e, align_bytes=64))
+                scales.append(keep.tile([P, C], U8, name="scales%d" % e, align_bytes=64))
+                nc.vector.quantize_mx(codes[e][:].bitcast(FP8X4), scales[e][:], grouped[:])
+
+            def back_first(e):
+                first = psum.tile([P, 2 * C], F32, name="first", bufs=1)
+                back(e, 0, first[:, 0:C])
+                if "SSSSSS"[e] == "S":
+                    nc.scalar.copy(dx[0][:, e * C : (e + 1) * C], first[:, 0:C])
+                else:
+                    nc.vector.tensor_copy(dx[0][:, e * C : (e + 1) * C], first[:, 0:C])
+
+            def finish_block(j):
+                e, b = divmod(j, BLOCKS)
+                bank = psum.tile([P, BLOCKS, 2, P], F32, name="turn", tag="turn", bufs=2)
+                for u in range(2):
+                    nc.tensor.transpose(bank[:, 0, u, :], das[j][u], ident[:])
+                grouped = work.tile([P, P * 4], BF16, name="grouped", align_bytes=64)
+                to = grouped[:].bitcast(F32).rearrange("p (s u) -> p s u", u=2)
+                if TEV[e] == "S":
+                    nc.scalar.copy(to, bank[:, 0].rearrange("p u s -> p s u"))
+                else:
+                    nc.vector.tensor_copy(to, bank[:, 0].rearrange("p u s -> p s u"))
+                if b == 0:
+                    codes.append(keep.tile([P, C], U32, name="codes%d" % e, align_bytes=64))
+                    scales.append(keep.tile([P, C], U8, name="scales%d" % e, align_bytes=64))
+                cols = slice(b * P, (b + 1) * P)
+                nc.vector.quantize_mx(codes[e][:, cols].bitcast(FP8X4), scales[e][:, cols], grouped[:])
+                first = psum.tile([P, 2 * C], F32, name="first", bufs=1)
+                nc.tensor.matmul_mx(
+                    first[:, 0:P], lhsT=w3w[e][:, 0 : P * WORD_BYTES].bitcast(FP4X4), lhsT_scale=w3s[:, e * K : e * K + P],
+                    rhs=codes[e][:, cols].bitcast(FP8X4), rhs_scale=scales[e][:, cols], start=True, stop=True,
+                )
+                if "SSSSSS"[e] == "S":
+                    nc.scalar.copy(dx[0][:, j * P : (j + 1) * P], first[:, 0:P])
+                else:
+                    nc.vector.tensor_copy(dx[0][:, j * P : (j + 1) * P], first[:, 0:P])
+
+            whole = (E - SPLIT) * BLOCKS
+            gather(0)
+            for step in range(E * BLOCKS + 6):
+                if step < E * BLOCKS:
+                    gradient(step)
+                if step % BLOCKS == 0 and step // BLOCKS + 1 < E:
+                    gather(step // BLOCKS + 1)
+                j = step - 2
+                if 0 <= j < whole:
+                    turn_block(j)
+                j = step - 2
+                if 0 <= j < whole and j % BLOCKS == 1:
+                    quantise(j // BLOCKS)
+                j = step - 4
+                if 0 <= j < whole and j % BLOCKS == 1:
+                    back_first(j // BLOCKS)
+            for j in range(whole, E * BLOCKS):
+                finish_block(j)
+
+        late = ctx.enter_context(tc.psum_pool(name="late", bufs=6))
+        for kb in range(K // P):
+            if kb > 0:
+                for e in range(0, E, 2):
+                    pair = late.tile([P, 2 * C], F32, name="pair")
+                    back(e, kb, pair[:, 0:C])
+                    back(e + 1, kb, pair[:, C : 2 * C])
+                    nc.scalar.copy(dx[kb][:, e * C : (e + 2) * C], pair[:])
+            cuts = (0, T) if kb < K // P - 1 else (0, 512, T)
+            for t0, t1 in zip(cuts, cuts[1:]):
+                width = t1 - t0
+                one = work.tile([P, T], F32, name="one")
+                two = work.tile([P, T], F32, name="two")
+                both = work.tile([P, T], F32, name="both")
+                picks = slice(t0 // LIST_ROWS, t1 // LIST_ROWS)
+                nc.vector.tensor_copy(one[:, 0:width], dx[kb][:].indirect(pos1_t[:, picks]))
+                nc.vector.tensor_copy(two[:, 0:width], dx[kb][:].indirect(pos2_t[:, picks]))
+                adder = nc.vector if ADDS[kb] == "V" or t1 == T and kb == K // P - 1 else nc.gpsimd
+                adder.tensor_tensor(both[:, 0:width], one[:, 0:width], two[:, 0:width], ALU.add)
+                nc.sync.dma_start(out[kb * P : (kb + 1) * P, t0:t1], both[:, 0:width])

@@ -23,13 +23,26 @@ LIST_ROWS = 16
 BLOCKS = C // P
 WORD_BYTES = 2
 EARLY = 2
-MODES = "AAAAAAAAAAAA"
-ADDS = "VVVV"
-TEV = "SSSSSS"
+MODES = "CCDBCCBBFFFA"
+ADDS = "GGGV"
+TEV = "VSSSSS"
 GROUPS = (0, 1, 2, 3, 4, 5, 6)
 WIDE = "000000"
 SPLIT = 1
-HEAD = 1
+HEAD = "oxgyX1AYB2"
+XB = 2
+YB = 2
+AB = 3
+HB = 2
+TB = 2
+FB = 1
+EB = 3
+LAGT = 3
+LAGE = 3
+LAGB = 5
+LAGG = 0
+DXEV = "SSSSSV"
+CUTS = (0, 512, T)
 
 
 def tile_moe_rec_mlp_silu_kernel(
@@ -85,28 +98,28 @@ def tile_moe_rec_mlp_silu_kernel(
             return [t[:, e, :] for e in range(e1 - e0)]
 
         gate_src = gate.rearrange("a (b p) -> (a b) p", p=P)[0:P, :]
-        nc.sync.dma_start(offs_t[:], offs)
-        load_token_words(xw, x_words)
-        if HEAD == 1:
-            w1w = load_weight_words(nc.sync, w1_words, 0, EARLY, "w1_early")
-            load_token_words(yw, dy_words)
-            load_token_scales(xs, x_scales)
-            load_weight_scales(w1s, w1_scales)
-            load_token_scales(ys, dy_scales)
-            load_weight_scales(w2s, w2t_scales)
-            w2w = load_weight_words(nc.sync, w2t_words, 0, EARLY, "w2_early")
-            nc.sync.dma_start(gate_rows[:], gate_src)
-            make_identity(nc, ident[:])
-        else:
-            w1w = load_weight_words(nc.gpsimd, w1_words, 0, EARLY, "w1_early")
-            w2w = load_weight_words(nc.gpsimd, w2t_words, 0, EARLY, "w2_early")
-            nc.gpsimd.dma_start(gate_rows[:], gate_src)
-            make_identity(nc, ident[:])
-            load_token_scales(xs, x_scales)
-            load_weight_scales(w1s, w1_scales)
-            load_token_words(yw, dy_words)
-            load_token_scales(ys, dy_scales)
-            load_weight_scales(w2s, w2t_scales)
+        make_identity(nc, ident[:])
+        for what in HEAD:
+            if what == "o":
+                nc.sync.dma_start(offs_t[:], offs)
+            elif what == "x":
+                load_token_words(xw, x_words)
+            elif what == "y":
+                load_token_words(yw, dy_words)
+            elif what == "g":
+                nc.sync.dma_start(gate_rows[:], gate_src)
+            elif what == "1":
+                w1w = load_weight_words(nc.sync, w1_words, 0, EARLY, "w1_early")
+            elif what == "2":
+                w2w = load_weight_words(nc.sync, w2t_words, 0, EARLY, "w2_early")
+            elif what == "X":
+                load_token_scales(xs, x_scales)
+            elif what == "Y":
+                load_token_scales(ys, dy_scales)
+            elif what == "A":
+                load_weight_scales(w1s, w1_scales)
+            else:
+                load_weight_scales(w2s, w2t_scales)
         w1w = w1w + load_weight_words(nc.sync, w1_words, EARLY, E, "w1_late")
         w2w = w2w + load_weight_words(nc.sync, w2t_words, EARLY, E, "w2_late")
         load_weight_scales(w3s, w1t_scales)
@@ -132,7 +145,7 @@ def tile_moe_rec_mlp_silu_kernel(
             return t[:].rearrange("s (u p d) -> s u p d", u=2, d=2)
 
         with tc.psum_pool(name="psum", bufs=2) as psum:
-            gate_ps = psum.tile([P, 4, P], F32, name="turn", tag="turn", bufs=2)
+            gate_ps = psum.tile([P, 4, P], F32, name="turn", tag="turn", bufs=TB)
             nc.tensor.transpose(gate_ps[:, 0, :], gate_rows[:], ident[:])
             nc.vector.tensor_scalar(gate_cols[:], gate_ps[:, 0, 0 : E * BLOCKS], -0.5, None, ALU.mult)
 
@@ -144,10 +157,10 @@ def tile_moe_rec_mlp_silu_kernel(
                 e1 = GROUPS[GROUPS.index(e) + 1]
                 n = (e1 - e) * C
                 slots = offs_t[:, e * C // LIST_ROWS : e1 * C // LIST_ROWS]
-                xg = picked.tile([P, n], U32, name="xg", align_bytes=64, bufs=2)
-                xgs = picked.tile([P, n], U8, name="xgs", align_bytes=64, bufs=2)
-                yg = picked.tile([P, n], U32, name="yg", align_bytes=64, bufs=2)
-                ygs = picked.tile([P, n], U8, name="ygs", align_bytes=64, bufs=2)
+                xg = picked.tile([P, n], U32, name="xg", align_bytes=64, bufs=XB)
+                xgs = picked.tile([P, n], U8, name="xgs", align_bytes=64, bufs=XB)
+                yg = picked.tile([P, n], U32, name="yg", align_bytes=64, bufs=YB)
+                ygs = picked.tile([P, n], U8, name="ygs", align_bytes=64, bufs=YB)
                 nc.vector.tensor_copy(xg[:], xw[:].bitcast(U32).indirect(slots))
                 nc.vector.tensor_copy(xgs[:], xs[:].indirect(slots))
                 nc.vector.tensor_copy(yg[:], yw[:].bitcast(U32).indirect(slots))
@@ -161,19 +174,19 @@ def tile_moe_rec_mlp_silu_kernel(
                 mode = MODES[j]
                 gcol = gate_cols[:, j : j + 1]
                 cols = slice(b * P, (b + 1) * P)
-                a_ps = psum.tile([P, H], F32, name="a_ps", bufs=3)
+                a_ps = psum.tile([P, H], F32, name="a_ps", bufs=AB)
                 nc.tensor.matmul_mx(
                     a_ps[:], lhsT=xg[:, cols].bitcast(FP8X4), lhsT_scale=xgs[:, cols],
                     rhs=w1w[e].bitcast(FP4X4), rhs_scale=w1s[:, e * H : (e + 1) * H], start=True, stop=True,
                 )
-                h_ps = psum.tile([P, H], F32, name="h_ps", bufs=2)
+                h_ps = psum.tile([P, H], F32, name="h_ps", bufs=HB)
                 nc.tensor.matmul_mx(
                     h_ps[:], lhsT=yg[:, cols].bitcast(FP8X4), lhsT_scale=ygs[:, cols],
                     rhs=w2w[e].bitcast(FP4X4), rhs_scale=w2s[:, e * H : (e + 1) * H], start=True, stop=True,
                 )
                 if b == 0:
-                    stage[e] = [work.tile([P, BLOCKS * H], F32, name=n, bufs=3) for n in ("silu", "tanh", "third", "part")]
-                    stage[e].append(work.tile([P, BLOCKS * H], BF16, name="da", bufs=3))
+                    stage[e] = [work.tile([P, BLOCKS * H], F32, name=n, bufs=EB) for n in ("silu", "tanh", "third", "part")]
+                    stage[e].append(work.tile([P, BLOCKS * H], BF16, name="da", bufs=EB))
                 silu, tanh, third, part, da = [t[:, b * H : (b + 1) * H] for t in stage[e]]
                 words = da.bitcast(F32)
                 wide = WIDE[e] == "1"
@@ -213,7 +226,7 @@ def tile_moe_rec_mlp_silu_kernel(
             def turn_block(j):
                 e, b = divmod(j, BLOCKS)
                 if b == 0:
-                    turns[e] = psum.tile([P, BLOCKS, 2, P], F32, name="turn", tag="turn", bufs=2)
+                    turns[e] = psum.tile([P, BLOCKS, 2, P], F32, name="turn", tag="turn", bufs=TB)
                 for u in range(2):
                     nc.tensor.transpose(turns[e][:, b, u, :], das[j][u], ident[:])
 
@@ -229,16 +242,16 @@ def tile_moe_rec_mlp_silu_kernel(
                 nc.vector.quantize_mx(codes[e][:].bitcast(FP8X4), scales[e][:], grouped[:])
 
             def back_first(e):
-                first = psum.tile([P, 2 * C], F32, name="first", bufs=1)
+                first = psum.tile([P, 2 * C], F32, name="first", bufs=FB)
                 back(e, 0, first[:, 0:C])
-                if "SSSSSS"[e] == "S":
+                if DXEV[e] == "S":
                     nc.scalar.copy(dx[0][:, e * C : (e + 1) * C], first[:, 0:C])
                 else:
                     nc.vector.tensor_copy(dx[0][:, e * C : (e + 1) * C], first[:, 0:C])
 
             def finish_block(j):
                 e, b = divmod(j, BLOCKS)
-                bank = psum.tile([P, BLOCKS, 2, P], F32, name="turn", tag="turn", bufs=2)
+                bank = psum.tile([P, BLOCKS, 2, P], F32, name="turn", tag="turn", bufs=TB)
                 for u in range(2):
                     nc.tensor.transpose(bank[:, 0, u, :], das[j][u], ident[:])
                 grouped = work.tile([P, P * 4], BF16, name="grouped", align_bytes=64)
@@ -252,12 +265,12 @@ def tile_moe_rec_mlp_silu_kernel(
                     scales.append(keep.tile([P, C], U8, name="scales%d" % e, align_bytes=64))
                 cols = slice(b * P, (b + 1) * P)
                 nc.vector.quantize_mx(codes[e][:, cols].bitcast(FP8X4), scales[e][:, cols], grouped[:])
-                first = psum.tile([P, 2 * C], F32, name="first", bufs=1)
+                first = psum.tile([P, 2 * C], F32, name="first", bufs=FB)
                 nc.tensor.matmul_mx(
                     first[:, 0:P], lhsT=w3w[e][:, 0 : P * WORD_BYTES].bitcast(FP4X4), lhsT_scale=w3s[:, e * K : e * K + P],
                     rhs=codes[e][:, cols].bitcast(FP8X4), rhs_scale=scales[e][:, cols], start=True, stop=True,
                 )
-                if "SSSSSS"[e] == "S":
+                if DXEV[e] == "S":
                     nc.scalar.copy(dx[0][:, j * P : (j + 1) * P], first[:, 0:P])
                 else:
                     nc.vector.tensor_copy(dx[0][:, j * P : (j + 1) * P], first[:, 0:P])
@@ -267,15 +280,15 @@ def tile_moe_rec_mlp_silu_kernel(
             for step in range(E * BLOCKS + 6):
                 if step < E * BLOCKS:
                     gradient(step)
-                if step % BLOCKS == 0 and step // BLOCKS + 1 < E:
+                if step % BLOCKS == LAGG and step // BLOCKS + 1 < E:
                     gather(step // BLOCKS + 1)
-                j = step - 2
+                j = step - LAGT
                 if 0 <= j < whole:
                     turn_block(j)
-                j = step - 2
+                j = step - LAGE
                 if 0 <= j < whole and j % BLOCKS == 1:
                     quantise(j // BLOCKS)
-                j = step - 4
+                j = step - LAGB
                 if 0 <= j < whole and j % BLOCKS == 1:
                     back_first(j // BLOCKS)
             for j in range(whole, E * BLOCKS):
@@ -289,7 +302,7 @@ def tile_moe_rec_mlp_silu_kernel(
                     back(e, kb, pair[:, 0:C])
                     back(e + 1, kb, pair[:, C : 2 * C])
                     nc.scalar.copy(dx[kb][:, e * C : (e + 2) * C], pair[:])
-            cuts = (0, T) if kb < K // P - 1 else (0, 512, T)
+            cuts = (0, T) if kb < K // P - 1 else CUTS
             for t0, t1 in zip(cuts, cuts[1:]):
                 width = t1 - t0
                 one = work.tile([P, T], F32, name="one")

@@ -23,25 +23,23 @@ LIST_ROWS = 16
 BLOCKS = C // P
 WORD_BYTES = 2
 EARLY = 2
-MODES = "CCDBCCBBFFFA"
-ADDS = "GGGV"
-TEV = "VSSSSS"
-GROUPS = (0, 1, 2, 3, 4, 5, 6)
+MODES = "HCCCCCBDBEFE"
+ADDS = "GGGG"
+TEV = "SSSSVS"
 WIDE = "000000"
 SPLIT = 1
-HEAD = "oxgyX1AYB2"
-XB = 2
-YB = 2
-AB = 3
-HB = 2
-TB = 2
-FB = 1
-EB = 3
+HEAD = "12ogXxAyYB"
+ZERO = "GVGVV"
+QUEUE = "SGG"
+PINS = "---326---235-01148--0035"
+SCE = 0
+PINT = 0
+PINF = 0
+EB = 4
 LAGT = 3
-LAGE = 3
-LAGB = 5
-LAGG = 0
-DXEV = "SSSSSV"
+LAGE = 5
+LAGB = 6
+DXEV = "VVSSVS"
 CUTS = (0, 512, T)
 
 
@@ -62,8 +60,17 @@ def tile_moe_rec_mlp_silu_kernel(
         yw = keep.tile([P, T], I32, name="yw", align_bytes=64)
         xs = keep.tile([P, T], U8, name="xs", align_bytes=64)
         ys = keep.tile([P, T], U8, name="ys", align_bytes=64)
-        w1s = keep.tile([P, E * H], U8, name="w1s", align_bytes=64)
-        w2s = keep.tile([P, E * H], U8, name="w2s", align_bytes=64)
+        w1s = keep.tile([P, (SCE or E) * H], U8, name="w1s", align_bytes=64)
+        w2s = keep.tile([P, (SCE or E) * H], U8, name="w2s", align_bytes=64)
+        w1v = [w1s[:, e * H : (e + 1) * H] for e in range(SCE or E)]
+        w2v = [w2s[:, e * H : (e + 1) * H] for e in range(SCE or E)]
+        planes = [xs, w1s, ys, w2s]
+        if SCE:
+            w1l = keep.tile([P, (E - SCE) * H], U8, name="w1l", align_bytes=64)
+            w2l = keep.tile([P, (E - SCE) * H], U8, name="w2l", align_bytes=64)
+            w1v = w1v + [w1l[:, e * H : (e + 1) * H] for e in range(E - SCE)]
+            w2v = w2v + [w2l[:, e * H : (e + 1) * H] for e in range(E - SCE)]
+            planes = planes + [w1l, w2l]
         w3s = keep.tile([P, E * K], U8, name="w3s", align_bytes=64)
         gate_rows = keep.tile([P, P], F32, name="gate_rows")
         gate_cols = keep.tile([P, E * BLOCKS], F32, name="gate_cols")
@@ -73,10 +80,8 @@ def tile_moe_rec_mlp_silu_kernel(
 
         nc.vector.memset(warm_in[:], 0.0)
         nc.scalar.activation(warm_out[:], warm_in[:], ACT.Silu)
-        for plane in (xs, ys):
-            nc.gpsimd.memset(plane[:].bitcast(I32), 0)
-        for plane in (w1s, w2s, w3s):
-            nc.vector.memset(plane[:].bitcast(I32), 0)
+        for plane, who in zip(planes + [w3s], ZERO[:4] + ZERO[4] * 3):
+            (nc.gpsimd if who == "G" else nc.vector).memset(plane[:].bitcast(I32), 0)
 
         def load_token_words(t, words):
             nc.sync.dma_start(t[:], words[0].rearrange("p t d -> p (t d)").bitcast(I32))
@@ -85,11 +90,11 @@ def tile_moe_rec_mlp_silu_kernel(
             for r in range(4):
                 nc.sync.dma_start(plane[:].bitcast(I32)[r:P:32, :], scales[0, r:16:4, :].bitcast(I32))
 
-        def load_weight_scales(plane, scales):
+        def load_weight_scales(plane, scales, e0, e1):
             for r in range(4):
                 nc.sync.dma_start(
-                    plane[:].bitcast(I32)[r:P:32, :].rearrange("q (e n) -> q e n", e=E),
-                    scales[:, 0, r:16:4, :].rearrange("e q n -> q e n").bitcast(I32),
+                    plane[:].bitcast(I32)[r:P:32, :].rearrange("q (e n) -> q e n", e=e1 - e0),
+                    scales[e0:e1, 0, r:16:4, :].rearrange("e q n -> q e n").bitcast(I32),
                 )
 
         def load_weight_words(queue, words, e0, e1, name):
@@ -98,34 +103,45 @@ def tile_moe_rec_mlp_silu_kernel(
             return [t[:, e, :] for e in range(e1 - e0)]
 
         gate_src = gate.rearrange("a (b p) -> (a b) p", p=P)[0:P, :]
-        make_identity(nc, ident[:])
+        queue = [nc.gpsimd if who == "G" else nc.sync for who in QUEUE]
         for what in HEAD:
             if what == "o":
                 nc.sync.dma_start(offs_t[:], offs)
+            elif what == "p":
+                nc.sync.dma_start(pos1_t[:], pos1)
+            elif what == "q":
+                nc.sync.dma_start(pos2_t[:], pos2)
             elif what == "x":
                 load_token_words(xw, x_words)
             elif what == "y":
                 load_token_words(yw, dy_words)
             elif what == "g":
-                nc.sync.dma_start(gate_rows[:], gate_src)
+                queue[0].dma_start(gate_rows[:], gate_src)
+                make_identity(nc, ident[:])
             elif what == "1":
-                w1w = load_weight_words(nc.sync, w1_words, 0, EARLY, "w1_early")
+                w1w = load_weight_words(queue[1], w1_words, 0, EARLY, "w1_early")
             elif what == "2":
-                w2w = load_weight_words(nc.sync, w2t_words, 0, EARLY, "w2_early")
+                w2w = load_weight_words(queue[2], w2t_words, 0, EARLY, "w2_early")
             elif what == "X":
                 load_token_scales(xs, x_scales)
             elif what == "Y":
                 load_token_scales(ys, dy_scales)
             elif what == "A":
-                load_weight_scales(w1s, w1_scales)
+                load_weight_scales(w1s, w1_scales, 0, SCE or E)
             else:
-                load_weight_scales(w2s, w2t_scales)
+                load_weight_scales(w2s, w2t_scales, 0, SCE or E)
+        if SCE:
+            load_weight_scales(w1l, w1_scales, SCE, E)
         w1w = w1w + load_weight_words(nc.sync, w1_words, EARLY, E, "w1_late")
+        if SCE:
+            load_weight_scales(w2l, w2t_scales, SCE, E)
         w2w = w2w + load_weight_words(nc.sync, w2t_words, EARLY, E, "w2_late")
-        load_weight_scales(w3s, w1t_scales)
+        load_weight_scales(w3s, w1t_scales, 0, E)
         w3w = load_weight_words(nc.sync, w1t_words, 0, E, "w3_all")
-        nc.sync.dma_start(pos1_t[:], pos1)
-        nc.sync.dma_start(pos2_t[:], pos2)
+        if "p" not in HEAD:
+            nc.sync.dma_start(pos1_t[:], pos1)
+        if "q" not in HEAD:
+            nc.sync.dma_start(pos2_t[:], pos2)
 
         dx = [keep.tile([P, S], F32, name="dx%d" % kb) for kb in range(K // P)]
         codes, scales = [], []
@@ -144,53 +160,74 @@ def tile_moe_rec_mlp_silu_kernel(
         def three(t):
             return t[:].rearrange("s (u p d) -> s u p d", u=2, d=2)
 
-        with tc.psum_pool(name="psum", bufs=2) as psum:
-            gate_ps = psum.tile([P, 4, P], F32, name="turn", tag="turn", bufs=TB)
+        with tc.psum_pool(name="psum", bufs=1) as psum:
+            order = list(range(8))
+            count = []
+
+            def bank(shape, newest=False):
+                b = order.pop(-1 if newest else 0)
+                count.append(b)
+                return psum.tile(shape, F32, name="bank%d" % len(count), offset=b * 2048), b
+
+            gate_ps, gate_bank = bank([P, 4, P])
+            order.append(gate_bank)
             nc.tensor.transpose(gate_ps[:, 0, :], gate_rows[:], ident[:])
             nc.vector.tensor_scalar(gate_cols[:], gate_ps[:, 0, 0 : E * BLOCKS], -0.5, None, ALU.mult)
 
-            picks, das, turns, stage = {}, {}, {}, {}
+            picks, das, turns, stage, held, used, usedb = {}, {}, {}, {}, {}, {}, {}
 
-            def gather(e):
-                if e not in GROUPS:
-                    return
-                e1 = GROUPS[GROUPS.index(e) + 1]
-                n = (e1 - e) * C
-                slots = offs_t[:, e * C // LIST_ROWS : e1 * C // LIST_ROWS]
-                xg = picked.tile([P, n], U32, name="xg", align_bytes=64, bufs=XB)
-                xgs = picked.tile([P, n], U8, name="xgs", align_bytes=64, bufs=XB)
-                yg = picked.tile([P, n], U32, name="yg", align_bytes=64, bufs=YB)
-                ygs = picked.tile([P, n], U8, name="ygs", align_bytes=64, bufs=YB)
-                nc.vector.tensor_copy(xg[:], xw[:].bitcast(U32).indirect(slots))
-                nc.vector.tensor_copy(xgs[:], xs[:].indirect(slots))
-                nc.vector.tensor_copy(yg[:], yw[:].bitcast(U32).indirect(slots))
-                nc.vector.tensor_copy(ygs[:], ys[:].indirect(slots))
-                for i in range(e, e1):
-                    picks[i] = [t[:, (i - e) * C : (i - e + 1) * C] for t in (xg, xgs, yg, ygs)]
+            def gather(sort, e, after):
+                window, dtype, at = ((xw[:].bitcast(U32), U32, 0), (xs[:], U8, 1024), (yw[:].bitcast(U32), U32, 0), (ys[:], U8, 1280))[sort]
+                slots = offs_t[:, e * C // LIST_ROWS : (e + 1) * C // LIST_ROWS]
+                name = "picked%d_%d" % (sort, e)
+                if after is None:
+                    t = keep.tile([P, C], dtype, name=name, align_bytes=64)
+                else:
+                    if dtype == U32:
+                        at = 1024 * used.get(after, 0)
+                        used[after] = 1 + used.get(after, 0)
+                    else:
+                        at = 2048 + 256 * usedb.get(after, 0)
+                        usedb[after] = 1 + usedb.get(after, 0)
+                    t = picked.tile([P, C], dtype, name=name, align_bytes=64, offset=after * 3072 + at)
+                nc.vector.tensor_copy(t[:], window.indirect(slots))
+                picks[sort, e] = t
+
+            def gathers(step):
+                for e in range(E):
+                    for sort in range(4):
+                        pin = PINS[sort * 6 + e]
+                        if pin == "-" and step == -1:
+                            gather(sort, e, None)
+                        elif pin != "-" and int(pin, 16) == step:
+                            gather(sort, e, step)
 
             def gradient(j):
                 e, b = divmod(j, BLOCKS)
-                xg, xgs, yg, ygs = picks[e]
+                xg, xgs, yg, ygs = [picks[sort, e] for sort in range(4)]
                 mode = MODES[j]
                 gcol = gate_cols[:, j : j + 1]
                 cols = slice(b * P, (b + 1) * P)
-                a_ps = psum.tile([P, H], F32, name="a_ps", bufs=AB)
+                a_ps, a_bank = bank([P, H])
                 nc.tensor.matmul_mx(
                     a_ps[:], lhsT=xg[:, cols].bitcast(FP8X4), lhsT_scale=xgs[:, cols],
-                    rhs=w1w[e].bitcast(FP4X4), rhs_scale=w1s[:, e * H : (e + 1) * H], start=True, stop=True,
+                    rhs=w1w[e].bitcast(FP4X4), rhs_scale=w1v[e], start=True, stop=True,
                 )
-                h_ps = psum.tile([P, H], F32, name="h_ps", bufs=HB)
+                h_ps, h_bank = bank([P, H])
+                order.extend([a_bank, h_bank])
                 nc.tensor.matmul_mx(
                     h_ps[:], lhsT=yg[:, cols].bitcast(FP8X4), lhsT_scale=ygs[:, cols],
-                    rhs=w2w[e].bitcast(FP4X4), rhs_scale=w2s[:, e * H : (e + 1) * H], start=True, stop=True,
+                    rhs=w2w[e].bitcast(FP4X4), rhs_scale=w2v[e], start=True, stop=True,
                 )
                 if b == 0:
-                    stage[e] = [work.tile([P, BLOCKS * H], F32, name=n, bufs=EB) for n in ("silu", "tanh", "third", "part")]
+                    stage[e] = [work.tile([P, BLOCKS * H], F32, name=n, bufs=EB) for n in ("tanh", "third", "part")]
                     stage[e].append(work.tile([P, BLOCKS * H], BF16, name="da", bufs=EB))
-                silu, tanh, third, part, da = [t[:, b * H : (b + 1) * H] for t in stage[e]]
+                tanh, third, part, da = [t[:, b * H : (b + 1) * H] for t in stage[e]]
+                silu_tile = picked.tile([P, 768], F32, name="silu%d" % j, align_bytes=64, offset=j * 3072)
+                silu = silu_tile[:, 0:H]
                 words = da.bitcast(F32)
                 wide = WIDE[e] == "1"
-                w_silu, w_tanh, w_third, w_part, w_da = stage[e]
+                w_tanh, w_third, w_part, w_da = stage[e]
                 if mode in "AF":
                     nc.scalar.activation(three(silu), by_word_parity(a_ps), ACT.Silu, scale=-1.0)
                     nc.scalar.activation(three(tanh), by_word_parity(a_ps), ACT.Tanh, scale=0.5)
@@ -203,20 +240,19 @@ def tile_moe_rec_mlp_silu_kernel(
                     else:
                         nc.vector.tensor_scalar(third[:], tanh[:], 1.0, gcol, ALU.add, ALU.mult)
                         nc.vector.tensor_tensor(three(part), three(third), by_word_parity(h_ps), ALU.mult)
-                    if not wide:
-                        nc.vector.scalar_tensor_tensor(da[:], silu[:], 1.0, part[:], ALU.subtract, ALU.mult)
-                    elif b == 1:
-                        nc.vector.scalar_tensor_tensor(w_da[:], w_silu[:], 1.0, w_part[:], ALU.subtract, ALU.mult)
+                    nc.vector.scalar_tensor_tensor(da[:], silu[:], 1.0, part[:], ALU.subtract, ALU.mult)
                     das[j] = [words[:, u * P : (u + 1) * P] for u in range(2)]
                 else:
                     nc.scalar.activation(silu[:], a_ps[:], ACT.Silu, scale=-1.0)
                     nc.scalar.activation(tanh[:], a_ps[:], ACT.Tanh, scale=0.5)
                     if mode in "CD":
                         nc.gpsimd.tensor_scalar(third[:], tanh[:], 1.0, gcol, ALU.add, ALU.mult)
+                    elif mode == "H":
+                        nc.vector.tensor_scalar(third[:], tanh[:], 1.0, gcol, ALU.add, ALU.mult)
                     else:
                         nc.scalar.activation(third[:], tanh[:], ACT.Identity, scale=gcol, bias=gcol)
                     nc.vector.scalar_tensor_tensor(part[:], silu[:], 1.0, h_ps[:], ALU.subtract, ALU.mult)
-                    last = nc.gpsimd if mode in "BC" else nc.vector
+                    last = nc.gpsimd if mode in "BCH" else nc.vector
                     if not wide:
                         last.tensor_tensor(da[:], part[:], third[:], ALU.mult)
                     elif b == 1:
@@ -226,7 +262,7 @@ def tile_moe_rec_mlp_silu_kernel(
             def turn_block(j):
                 e, b = divmod(j, BLOCKS)
                 if b == 0:
-                    turns[e] = psum.tile([P, BLOCKS, 2, P], F32, name="turn", tag="turn", bufs=TB)
+                    turns[e], held[e] = bank([P, BLOCKS, 2, P], PINT == 1)
                 for u in range(2):
                     nc.tensor.transpose(turns[e][:, b, u, :], das[j][u], ident[:])
 
@@ -237,12 +273,14 @@ def tile_moe_rec_mlp_silu_kernel(
                     nc.scalar.copy(to, turns[e][:].rearrange("p b u s -> p b s u"))
                 else:
                     nc.vector.tensor_copy(to, turns[e][:].rearrange("p b u s -> p b s u"))
+                order.insert(max(0, len(order) - 2), held[e])
                 codes.append(keep.tile([P, C], U32, name="codes%d" % e, align_bytes=64))
                 scales.append(keep.tile([P, C], U8, name="scales%d" % e, align_bytes=64))
                 nc.vector.quantize_mx(codes[e][:].bitcast(FP8X4), scales[e][:], grouped[:])
 
             def back_first(e):
-                first = psum.tile([P, 2 * C], F32, name="first", bufs=FB)
+                first, first_bank = bank([P, 2 * C], PINF == 1 and e < E - 1 - SPLIT)
+                order.append(first_bank)
                 back(e, 0, first[:, 0:C])
                 if DXEV[e] == "S":
                     nc.scalar.copy(dx[0][:, e * C : (e + 1) * C], first[:, 0:C])
@@ -251,21 +289,23 @@ def tile_moe_rec_mlp_silu_kernel(
 
             def finish_block(j):
                 e, b = divmod(j, BLOCKS)
-                bank = psum.tile([P, BLOCKS, 2, P], F32, name="turn", tag="turn", bufs=TB)
+                turn, turn_bank = bank([P, BLOCKS, 2, P])
+                order.append(turn_bank)
                 for u in range(2):
-                    nc.tensor.transpose(bank[:, 0, u, :], das[j][u], ident[:])
+                    nc.tensor.transpose(turn[:, 0, u, :], das[j][u], ident[:])
                 grouped = work.tile([P, P * 4], BF16, name="grouped", align_bytes=64)
                 to = grouped[:].bitcast(F32).rearrange("p (s u) -> p s u", u=2)
                 if TEV[e] == "S":
-                    nc.scalar.copy(to, bank[:, 0].rearrange("p u s -> p s u"))
+                    nc.scalar.copy(to, turn[:, 0].rearrange("p u s -> p s u"))
                 else:
-                    nc.vector.tensor_copy(to, bank[:, 0].rearrange("p u s -> p s u"))
+                    nc.vector.tensor_copy(to, turn[:, 0].rearrange("p u s -> p s u"))
                 if b == 0:
                     codes.append(keep.tile([P, C], U32, name="codes%d" % e, align_bytes=64))
                     scales.append(keep.tile([P, C], U8, name="scales%d" % e, align_bytes=64))
                 cols = slice(b * P, (b + 1) * P)
                 nc.vector.quantize_mx(codes[e][:, cols].bitcast(FP8X4), scales[e][:, cols], grouped[:])
-                first = psum.tile([P, 2 * C], F32, name="first", bufs=FB)
+                first, first_bank = bank([P, 2 * C])
+                order.append(first_bank)
                 nc.tensor.matmul_mx(
                     first[:, 0:P], lhsT=w3w[e][:, 0 : P * WORD_BYTES].bitcast(FP4X4), lhsT_scale=w3s[:, e * K : e * K + P],
                     rhs=codes[e][:, cols].bitcast(FP8X4), rhs_scale=scales[e][:, cols], start=True, stop=True,
@@ -276,12 +316,11 @@ def tile_moe_rec_mlp_silu_kernel(
                     nc.vector.tensor_copy(dx[0][:, j * P : (j + 1) * P], first[:, 0:P])
 
             whole = (E - SPLIT) * BLOCKS
-            gather(0)
+            gathers(-1)
             for step in range(E * BLOCKS + 6):
                 if step < E * BLOCKS:
                     gradient(step)
-                if step % BLOCKS == LAGG and step // BLOCKS + 1 < E:
-                    gather(step // BLOCKS + 1)
+                    gathers(step)
                 j = step - LAGT
                 if 0 <= j < whole:
                     turn_block(j)

from contextlib import ExitStack

import concourse.mybir as mybir
from concourse.masks import make_identity

K, T, E, C, H, N = 512, 768, 6, 256, 512, 512
S = E * C
FLOPS = 3 * 2 * 512 * 512 * S

F32 = mybir.dt.float32
BF16 = mybir.dt.bfloat16
I32 = mybir.dt.int32
U32 = mybir.dt.uint32
U16 = mybir.dt.uint16
U8 = mybir.dt.uint8
FP8X4 = mybir.dt.float8_e4m3fn_x4
FP4X4 = mybir.dt.float4_e2m1fn_x4
ACT = mybir.ActivationFunctionType
ALU = mybir.AluOpType

P = 128
LIST_ROWS = 16
BLOCKS = C // P
WORD_BYTES = 2
EARLY = 2
MODES = "HCCCCCBDBEFE"
ADDS = "GGGG"
TEV = "SSSSVS"
WIDE = "000000"
SPLIT = 1
HEAD = "12ogXxAyYB"
ZERO = "GVGVV"
QUEUE = "SGG"
PINS = "---326---235-01148--0035"
SCE = 0
PINT = 0
PINF = 0
EB = 4
LAGT = 3
LAGE = 5
LAGB = 6
DXEV = "VVSSVS"
CUTS = (0, 512, T)


def tile_moe_rec_mlp_silu_kernel(
    tc, x_words, x_scales, dy_words, dy_scales, w1_words, w1_scales, w2t_words, w2t_scales,
    w1t_words, w1t_scales, gate, offs, pos1, pos2, out,
):
    nc = tc.nc
    with ExitStack() as ctx:
        keep = ctx.enter_context(tc.tile_pool(name="keep", bufs=1))
        work = ctx.enter_context(tc.tile_pool(name="work", bufs=4))
        picked = ctx.enter_context(tc.tile_pool(name="picked", bufs=1))

        offs_t = keep.tile([P, S // LIST_ROWS], U16, name="offs_t")
        pos1_t = keep.tile([P, T // LIST_ROWS], U16, name="pos1_t")
        pos2_t = keep.tile([P, T // LIST_ROWS], U16, name="pos2_t")
        xw = keep.tile([P, T], I32, name="xw", align_bytes=64)
        yw = keep.tile([P, T], I32, name="yw", align_bytes=64)
        xs = keep.tile([P, T], U8, name="xs", align_bytes=64)
        ys = keep.tile([P, T], U8, name="ys", align_bytes=64)
        w1s = keep.tile([P, (SCE or E) * H], U8, name="w1s", align_bytes=64)
        w2s = keep.tile([P, (SCE or E) * H], U8, name="w2s", align_bytes=64)
        w1v = [w1s[:, e * H : (e + 1) * H] for e in range(SCE or E)]
        w2v = [w2s[:, e * H : (e + 1) * H] for e in range(SCE or E)]
        planes = [xs, w1s, ys, w2s]
        if SCE:
            w1l = keep.tile([P, (E - SCE) * H], U8, name="w1l", align_bytes=64)
            w2l = keep.tile([P, (E - SCE) * H], U8, name="w2l", align_bytes=64)
            w1v = w1v + [w1l[:, e * H : (e + 1) * H] for e in range(E - SCE)]
            w2v = w2v + [w2l[:, e * H : (e + 1) * H] for e in range(E - SCE)]
            planes = planes + [w1l, w2l]
        w3s = keep.tile([P, E * K], U8, name="w3s", align_bytes=64)
        gate_rows = keep.tile([P, P], F32, name="gate_rows")
        gate_cols = keep.tile([P, E * BLOCKS], F32, name="gate_cols")
        ident = keep.tile([P, P], F32, name="ident")
        warm_in = keep.tile([P, 1], F32, name="warm_in")
        warm_out = keep.tile([P, 1], F32, name="warm_out")

        nc.vector.memset(warm_in[:], 0.0)
        nc.scalar.activation(warm_out[:], warm_in[:], ACT.Silu)
        for plane, who in zip(planes + [w3s], ZERO[:4] + ZERO[4] * 3):
            (nc.gpsimd if who == "G" else nc.vector).memset(plane[:].bitcast(I32), 0)

        def load_token_words(t, words):
            nc.sync.dma_start(t[:], words[0].rearrange("p t d -> p (t d)").bitcast(I32))

        def load_token_scales(plane, scales):
            for r in range(4):
                nc.sync.dma_start(plane[:].bitcast(I32)[r:P:32, :], scales[0, r:16:4, :].bitcast(I32))

        def load_weight_scales(plane, scales, e0, e1):
            for r in range(4):
                nc.sync.dma_start(
                    plane[:].bitcast(I32)[r:P:32, :].rearrange("q (e n) -> q e n", e=e1 - e0),
                    scales[e0:e1, 0, r:16:4, :].rearrange("e q n -> q e n").bitcast(I32),
                )

        def load_weight_words(queue, words, e0, e1, name):
            t = keep.tile([P, e1 - e0, H * WORD_BYTES], U8, name=name, align_bytes=64)
            queue.dma_start(t[:].bitcast(I32), words[e0:e1, 0].rearrange("e p n -> p e n").bitcast(I32))
            return [t[:, e, :] for e in range(e1 - e0)]

        gate_src = gate.rearrange("a (b p) -> (a b) p", p=P)[0:P, :]
        queue = [nc.gpsimd if who == "G" else nc.sync for who in QUEUE]
        for what in HEAD:
            if what == "o":
                nc.sync.dma_start(offs_t[:], offs)
            elif what == "p":
                nc.sync.dma_start(pos1_t[:], pos1)
            elif what == "q":
                nc.sync.dma_start(pos2_t[:], pos2)
            elif what == "x":
                load_token_words(xw, x_words)
            elif what == "y":
                load_token_words(yw, dy_words)
            elif what == "g":
                queue[0].dma_start(gate_rows[:], gate_src)
                make_identity(nc, ident[:])
            elif what == "1":
                w1w = load_weight_words(queue[1], w1_words, 0, EARLY, "w1_early")
            elif what == "2":
                w2w = load_weight_words(queue[2], w2t_words, 0, EARLY, "w2_early")
            elif what == "X":
                load_token_scales(xs, x_scales)
            elif what == "Y":
                load_token_scales(ys, dy_scales)
            elif what == "A":
                load_weight_scales(w1s, w1_scales, 0, SCE or E)
            else:
                load_weight_scales(w2s, w2t_scales, 0, SCE or E)
        if SCE:
            load_weight_scales(w1l, w1_scales, SCE, E)
        w1w = w1w + load_weight_words(nc.sync, w1_words, EARLY, E, "w1_late")
        if SCE:
            load_weight_scales(w2l, w2t_scales, SCE, E)
        w2w = w2w + load_weight_words(nc.sync, w2t_words, EARLY, E, "w2_late")
        load_weight_scales(w3s, w1t_scales, 0, E)
        w3w = load_weight_words(nc.sync, w1t_words, 0, E, "w3_all")
        if "p" not in HEAD:
            nc.sync.dma_start(pos1_t[:], pos1)
        if "q" not in HEAD:
            nc.sync.dma_start(pos2_t[:], pos2)

        dx = [keep.tile([P, S], F32, name="dx%d" % kb) for kb in range(K // P)]
        codes, scales = [], []

        def back(e, kb, bank):
            nc.tensor.matmul_mx(
                bank,
                lhsT=w3w[e][:, kb * P * WORD_BYTES : (kb + 1) * P * WORD_BYTES].bitcast(FP4X4),
                lhsT_scale=w3s[:, e * K + kb * P : e * K + (kb + 1) * P],
                rhs=codes[e][:].bitcast(FP8X4), rhs_scale=scales[e][:], start=True, stop=True,
            )

        def by_word_parity(bank):
            return bank[:].rearrange("s (p u d) -> s u p d", u=2, d=2)

        def three(t):
            return t[:].rearrange("s (u p d) -> s u p d", u=2, d=2)

        with tc.psum_pool(name="psum", bufs=1) as psum:
            order = list(range(8))
            count = []

            def bank(shape, newest=False):
                b = order.pop(-1 if newest else 0)
                count.append(b)
                return psum.tile(shape, F32, name="bank%d" % len(count), offset=b * 2048), b

            gate_ps, gate_bank = bank([P, 4, P])
            order.append(gate_bank)
            nc.tensor.transpose(gate_ps[:, 0, :], gate_rows[:], ident[:])
            nc.vector.tensor_scalar(gate_cols[:], gate_ps[:, 0, 0 : E * BLOCKS], -0.5, None, ALU.mult)

            picks, das, turns, stage, held, used, usedb = {}, {}, {}, {}, {}, {}, {}

            def gather(sort, e, after):
                window, dtype, at = ((xw[:].bitcast(U32), U32, 0), (xs[:], U8, 1024), (yw[:].bitcast(U32), U32, 0), (ys[:], U8, 1280))[sort]
                slots = offs_t[:, e * C // LIST_ROWS : (e + 1) * C // LIST_ROWS]
                name = "picked%d_%d" % (sort, e)
                if after is None:
                    t = keep.tile([P, C], dtype, name=name, align_bytes=64)
                else:
                    if dtype == U32:
                        at = 1024 * used.get(after, 0)
                        used[after] = 1 + used.get(after, 0)
                    else:
                        at = 2048 + 256 * usedb.get(after, 0)
                        usedb[after] = 1 + usedb.get(after, 0)
                    t = picked.tile([P, C], dtype, name=name, align_bytes=64, offset=after * 3072 + at)
                nc.vector.tensor_copy(t[:], window.indirect(slots))
                picks[sort, e] = t

            def gathers(step):
                for e in range(E):
                    for sort in range(4):
                        pin = PINS[sort * 6 + e]
                        if pin == "-" and step == -1:
                            gather(sort, e, None)
                        elif pin != "-" and int(pin, 16) == step:
                            gather(sort, e, step)

            def gradient(j):
                e, b = divmod(j, BLOCKS)
                xg, xgs, yg, ygs = [picks[sort, e] for sort in range(4)]
                mode = MODES[j]
                gcol = gate_cols[:, j : j + 1]
                cols = slice(b * P, (b + 1) * P)
                a_ps, a_bank = bank([P, H])
                nc.tensor.matmul_mx(
                    a_ps[:], lhsT=xg[:, cols].bitcast(FP8X4), lhsT_scale=xgs[:, cols],
                    rhs=w1w[e].bitcast(FP4X4), rhs_scale=w1v[e], start=True, stop=True,
                )
                h_ps, h_bank = bank([P, H])
                order.extend([a_bank, h_bank])
                nc.tensor.matmul_mx(
                    h_ps[:], lhsT=yg[:, cols].bitcast(FP8X4), lhsT_scale=ygs[:, cols],
                    rhs=w2w[e].bitcast(FP4X4), rhs_scale=w2v[e], start=True, stop=True,
                )
                if b == 0:
                    stage[e] = [work.tile([P, BLOCKS * H], F32, name=n, bufs=EB) for n in ("tanh", "third", "part")]
                    stage[e].append(work.tile([P, BLOCKS * H], BF16, name="da", bufs=EB))
                tanh, third, part, da = [t[:, b * H : (b + 1) * H] for t in stage[e]]
                silu_tile = picked.tile([P, 768], F32, name="silu%d" % j, align_bytes=64, offset=j * 3072)
                silu = silu_tile[:, 0:H]
                words = da.bitcast(F32)
                wide = WIDE[e] == "1"
                w_tanh, w_third, w_part, w_da = stage[e]
                if mode in "AF":
                    nc.scalar.activation(three(silu), by_word_parity(a_ps), ACT.Silu, scale=-1.0)
                    nc.scalar.activation(three(tanh), by_word_parity(a_ps), ACT.Tanh, scale=0.5)
                    if mode == "A":
                        nc.scalar.activation(three(third), by_word_parity(h_ps), ACT.Copy, scale=gcol)
                        if not wide:
                            nc.vector.scalar_tensor_tensor(part[:], tanh[:], 1.0, third[:], ALU.add, ALU.mult)
                        elif b == 1:
                            nc.vector.scalar_tensor_tensor(w_part[:], w_tanh[:], 1.0, w_third[:], ALU.add, ALU.mult)
                    else:
                        nc.vector.tensor_scalar(third[:], tanh[:], 1.0, gcol, ALU.add, ALU.mult)
                        nc.vector.tensor_tensor(three(part), three(third), by_word_parity(h_ps), ALU.mult)
                    nc.vector.scalar_tensor_tensor(da[:], silu[:], 1.0, part[:], ALU.subtract, ALU.mult)
                    das[j] = [words[:, u * P : (u + 1) * P] for u in range(2)]
                else:
                    nc.scalar.activation(silu[:], a_ps[:], ACT.Silu, scale=-1.0)
                    nc.scalar.activation(tanh[:], a_ps[:], ACT.Tanh, scale=0.5)
                    if mode in "CD":
                        nc.gpsimd.tensor_scalar(third[:], tanh[:], 1.0, gcol, ALU.add, ALU.mult)
                    elif mode == "H":
                        nc.vector.tensor_scalar(third[:], tanh[:], 1.0, gcol, ALU.add, ALU.mult)
                    else:
                        nc.scalar.activation(third[:], tanh[:], ACT.Identity, scale=gcol, bias=gcol)
                    nc.vector.scalar_tensor_tensor(part[:], silu[:], 1.0, h_ps[:], ALU.subtract, ALU.mult)
                    last = nc.gpsimd if mode in "BCH" else nc.vector
                    if not wide:
                        last.tensor_tensor(da[:], part[:], third[:], ALU.mult)
                    elif b == 1:
                        last.tensor_tensor(w_da[:], w_part[:], w_third[:], ALU.mult)
                    das[j] = [words[:, u : 2 * P : 2] for u in range(2)]

            def turn_block(j):
                e, b = divmod(j, BLOCKS)
                if b == 0:
                    turns[e], held[e] = bank([P, BLOCKS, 2, P], PINT == 1)
                for u in range(2):
                    nc.tensor.transpose(turns[e][:, b, u, :], das[j][u], ident[:])

            def quantise(e):
                grouped = work.tile([P, C * 4], BF16, name="grouped", align_bytes=64)
                to = grouped[:].bitcast(F32).rearrange("p (b s u) -> p b s u", b=BLOCKS, u=2)
                if TEV[e] == "S":
                    nc.scalar.copy(to, turns[e][:].rearrange("p b u s -> p b s u"))
                else:
                    nc.vector.tensor_copy(to, turns[e][:].rearrange("p b u s -> p b s u"))
                order.insert(max(0, len(order) - 2), held[e])
                codes.append(keep.tile([P, C], U32, name="codes%d" % e, align_bytes=64))
                scales.append(keep.tile([P, C], U8, name="scales%d" % e, align_bytes=64))
                nc.vector.quantize_mx(codes[e][:].bitcast(FP8X4), scales[e][:], grouped[:])

            def back_first(e):
                first, first_bank = bank([P, 2 * C], PINF == 1 and e < E - 1 - SPLIT)
                order.append(first_bank)
                back(e, 0, first[:, 0:C])
                if DXEV[e] == "S":
                    nc.scalar.copy(dx[0][:, e * C : (e + 1) * C], first[:, 0:C])
                else:
                    nc.vector.tensor_copy(dx[0][:, e * C : (e + 1) * C], first[:, 0:C])

            def finish_block(j):
                e, b = divmod(j, BLOCKS)
                turn, turn_bank = bank([P, BLOCKS, 2, P])
                order.append(turn_bank)
                for u in range(2):
                    nc.tensor.transpose(turn[:, 0, u, :], das[j][u], ident[:])
                grouped = work.tile([P, P * 4], BF16, name="grouped", align_bytes=64)
                to = grouped[:].bitcast(F32).rearrange("p (s u) -> p s u", u=2)
                if TEV[e] == "S":
                    nc.scalar.copy(to, turn[:, 0].rearrange("p u s -> p s u"))
                else:
                    nc.vector.tensor_copy(to, turn[:, 0].rearrange("p u s -> p s u"))
                if b == 0:
                    codes.append(keep.tile([P, C], U32, name="codes%d" % e, align_bytes=64))
                    scales.append(keep.tile([P, C], U8, name="scales%d" % e, align_bytes=64))
                cols = slice(b * P, (b + 1) * P)
                nc.vector.quantize_mx(codes[e][:, cols].bitcast(FP8X4), scales[e][:, cols], grouped[:])
                first, first_bank = bank([P, 2 * C])
                order.append(first_bank)
                nc.tensor.matmul_mx(
                    first[:, 0:P], lhsT=w3w[e][:, 0 : P * WORD_BYTES].bitcast(FP4X4), lhsT_scale=w3s[:, e * K : e * K + P],
                    rhs=codes[e][:, cols].bitcast(FP8X4), rhs_scale=scales[e][:, cols], start=True, stop=True,
                )
                if DXEV[e] == "S":
                    nc.scalar.copy(dx[0][:, j * P : (j + 1) * P], first[:, 0:P])
                else:
                    nc.vector.tensor_copy(dx[0][:, j * P : (j + 1) * P], first[:, 0:P])

            whole = (E - SPLIT) * BLOCKS
            gathers(-1)
            for step in range(E * BLOCKS + 6):
                if step < E * BLOCKS:
                    gradient(step)
                    gathers(step)
                j = step - LAGT
                if 0 <= j < whole:
                    turn_block(j)
                j = step - LAGE
                if 0 <= j < whole and j % BLOCKS == 1:
                    quantise(j // BLOCKS)
                j = step - LAGB
                if 0 <= j < whole and j % BLOCKS == 1:
                    back_first(j // BLOCKS)
            for j in range(whole, E * BLOCKS):
                finish_block(j)

        late = ctx.enter_context(tc.psum_pool(name="late", bufs=6))
        for kb in range(K // P):
            if kb > 0:
                for e in range(0, E, 2):
                    pair = late.tile([P, 2 * C], F32, name="pair")
                    back(e, kb, pair[:, 0:C])
                    back(e + 1, kb, pair[:, C : 2 * C])
                    nc.scalar.copy(dx[kb][:, e * C : (e + 2) * C], pair[:])
            cuts = (0, T) if kb < K // P - 1 else CUTS
            for t0, t1 in zip(cuts, cuts[1:]):
                width = t1 - t0
                one = work.tile([P, T], F32, name="one")
                two = work.tile([P, T], F32, name="two")
                both = work.tile([P, T], F32, name="both")
                picks = slice(t0 // LIST_ROWS, t1 // LIST_ROWS)
                nc.vector.tensor_copy(one[:, 0:width], dx[kb][:].indirect(pos1_t[:, picks]))
                nc.vector.tensor_copy(two[:, 0:width], dx[kb][:].indirect(pos2_t[:, picks]))
                adder = nc.vector if ADDS[kb] == "V" or t1 == T and kb == K // P - 1 else nc.gpsimd
                adder.tensor_tensor(both[:, 0:width], one[:, 0:width], two[:, 0:width], ALU.add)
                nc.sync.dma_start(out[kb * P : (kb + 1) * P, t0:t1], both[:, 0:width])
